import numpy as np, ml_dtypes
CORES = [49,52,55,57,60,63,65,68,71,73,76,79]
N = 12
R, T = 4096, 512
CAPP = 128
def entries(a): return a.T.reshape(-1)
def pack(v, P): return np.ascontiguousarray(np.asarray(v, np.int32).reshape(-1, P).T)
def lists(rng, how):
    I = rng.integers(0, N * R, (N, T))
    O = np.stack([rng.permutation(np.repeat(np.arange(N), CAPP))[:T] for r in range(N)])
    if how == "full": O = np.stack([rng.permutation(np.repeat(rng.permutation(N)[:T // CAPP], CAPP)) for r in range(N)])
    I = R * O + rng.integers(0, R, (N, T))
    if how == "alike": I = R * O + rng.integers(0, R, (N, 1))
    if how == "edge": I = R * O + np.where(rng.random((N, T)) < 0.5, 0, R - 1)
    if how == "sorted": I = np.sort(I, axis=1)
    return {"idx": np.stack([pack(I[r], 16) for r in range(N)])}
def setup_inputs(rng):
    return dict({"tab": rng.standard_normal((N, 128, R), dtype=np.float32).astype(ml_dtypes.bfloat16)}, **lists(rng, "uniform"))
def setup_inputs_alike(rng):
    d = setup_inputs(rng); d.update(lists(rng, "alike"))
    for k in ("tab",): d[k] = (d[k].astype(np.float32) * 1048576.0).astype(d[k].dtype)
    return d
def setup_inputs_edge(rng):
    d = setup_inputs(rng); d.update(lists(rng, "edge"))
    for k in ("tab",): d[k] = (d[k].astype(np.float32) * (1 / 1024.0)).astype(d[k].dtype)
    return d
def setup_inputs_full(rng):
    d = setup_inputs(rng); d.update(lists(rng, "full"))
    return d
def setup_inputs_sorted(rng):
    d = setup_inputs(rng); d.update(lists(rng, "sorted"))
    return d
def check_inputs(x):
    bad = []
    if x["idx"].min() < 0 or x["idx"].max() >= N * R: bad.append("idx out of range")
    if max(int(np.bincount(entries(a) // R, minlength=N).max()) for a in x["idx"]) > CAPP: bad.append("more than CAPP entries of a list point into one rank's part")
    return bad
def reference(tab, idx):
    A = np.concatenate(list(tab), axis=1)
    return {"y": np.stack([A[:, entries(idx[r])] for r in range(N)])}

@@ -1,0 +1,348 @@
+from concourse.bass import DstId, RemoteDMATransfer
+from concourse.mybir import AluOpType, AxisListType
+
+RCOL = 4096
+CAP = 128
+NENT = 512
+W8 = CAP // 16
+
+SCRATCH = {
+    "tabS": ("sbuf", [128, RCOL], "bfloat16"),
+    "e_i": ("sbuf", [128, 4], "int32"),
+    "ol_i": ("sbuf", [128, 8], "int32"),
+    "ol_f": ("sbuf", [128, 8], "float32"),
+    "opad": ("sbuf", [128, 84], "bfloat16"),
+    "ones_b": ("sbuf", [128, 128], "bfloat16"),
+    "ut": ("sbuf", [128, 128], "bfloat16"),
+    "rowc": ("sbuf", [128, 48], "bfloat16"),
+    "io96": ("sbuf", [128, 96], "float32"),
+    "iom16": ("sbuf", [128, 128], "float32"),
+    "ioc4": ("sbuf", [128, 32], "float32"),
+    "p_i": ("sbuf", [128, 1], "int32"),
+    "pc_i": ("sbuf", [128, 2], "int32"),
+    "pc_f": ("sbuf", [128, 2], "float32"),
+    "mk": ("sbuf", [128, 32], "float32"),
+    "l2": ("sbuf", [128, 128], "float32"),
+    "tmpv": ("sbuf", [128, 48], "float32"),
+    "pos_f": ("sbuf", [128, 4], "float32"),
+    "pos_i": ("sbuf", [128, 4], "int32"),
+    "hl_i": ("sbuf", [128, 8], "int32"),
+    "hl_f": ("sbuf", [128, 8], "float32"),
+    "amat": ("sbuf", [128, 512], "float32"),
+    "bmat": ("sbuf", [128, 384], "float32"),
+    "req": ("sbuf", [128, 96], "uint16"),
+    "rhs2": ("sbuf", [128, 32], "float32"),
+    "posoff": ("sbuf", [128, 32], "uint16"),
+    "gw": ("sbuf", [128, 72], "uint16"),
+    "rq": ("sbuf", [128, 288], "uint16"),
+    "rep": ("sbuf", [128, 1536], "bfloat16"),
+    "land": ("sbuf", [128, 1536], "bfloat16"),
+    "yS": ("sbuf", [128, NENT], "bfloat16"),
+    "cnt_ps": ("psum", [128, 512], "float32"),
+    "rq_ps": ("psum", [128, 512], "float32"),
+    "po_ps": ("psum", [128, 512], "float32"),
+}
+SEMAPHORES = (["s_idx", "s_tab", "s_ms", "cga", "cgb", "k1", "k2", "k3"]
+              + ["s%d" % i for i in range(1, 16)]
+              + ["gwin", "tabin", "rq0", "rq1", "rq2", "rq3", "got", "sent", "selfg", "fin", "ydone"]
+              + ["gth%d" % i for i in range(6)])
+
+
+def _bits(m):
+    return [b for b in range(32) if (m >> b) & 1]
+
+
+def _mk(eng):
+    return sum(1 << b for b in eng)
+
+
+def _plan(cores, topo):
+    chips = []
+    for c in cores:
+        if topo.chip(c) not in chips:
+            chips.append(topo.chip(c))
+    allc = range(max(cores) + 1)
+    on = {X: [c for c in allc if topo.chip(c) == X] for X in chips}
+    rk = {X: [c for c in cores if topo.chip(c) == X] for X in chips}
+    m = len(rk[chips[0]])
+    for ci, X in enumerate(chips):
+        assert len(rk[X]) == m
+        for i, c in enumerate(rk[X]):
+            assert cores.index(c) == ci * m + i
+
+    def rel(X, Y):
+        if X == Y:
+            return "own"
+        if topo.mates(X, Y):
+            return "mate"
+        if topo.same_plane(X, Y):
+            return "plane"
+        return "hop2"
+
+    serv, helper, gate = {}, {}, {}
+    for X in chips:
+        far = rk[[Y for Y in chips if topo.mates(X, Y)][0]][0]
+        ports = [c for c in on[X] if topo.may_write(c, far)]
+        used = []
+        for k in sorted(range(m), key=lambda k: rk[X][k] in ports):
+            c = rk[X][k]
+            free = [h for h in on[X] if h not in rk[X] and h not in used]
+            if c in ports:
+                h = sorted(free, key=lambda h: (topo.die(h) != topo.die(c), h in ports, h))[0]
+                serv[(X, k)] = {"own": c, "plane": h, "mate": c, "hop2": c}
+            else:
+                h = sorted([h for h in free if h in ports], key=lambda h: (topo.die(h) != topo.die(c), h))[0]
+                serv[(X, k)] = {"own": c, "plane": c, "mate": h, "hop2": h}
+            used.append(h)
+            helper[(X, k)] = h
+        gs = [helper[(X, k)] for k in range(m) if helper[(X, k)] in ports]
+        assert len(gs) >= 2
+        gate[X] = {"mate": gs[0], "hop2": gs[1]}
+    return {"chips": chips, "on": on, "rk": rk, "m": m, "rel": rel, "serv": serv, "helper": helper, "gate": gate}
+
+
+def _engines(core, PL, topo):
+    X = topo.chip(core)
+    near = [c for c in PL["on"][X] if c != core][0]
+    far = PL["rk"][[Y for Y in PL["chips"] if Y != X][0]][0]
+    lo = _bits(topo.mask(core, far))
+    hi = [b for b in _bits(topo.mask(core, near)) if b not in lo]
+    return lo, hi
+
+
+def _table_of(core, PL, topo):
+    X = topo.chip(core)
+    for k in range(PL["m"]):
+        if PL["rk"][X][k] == core or PL["helper"][(X, k)] == core:
+            return k
+    return None
+
+
+def _sched(core, PL, topo):
+    Y = topo.chip(core)
+    k = _table_of(core, PL, topo)
+    if k is None:
+        return []
+    lo, hi = _engines(core, PL, topo)
+    sv = PL["serv"][(Y, k)]
+    calls = []
+    if sv["own"] == core:
+        own = [(Y, i) for i in range(PL["m"]) if i != k]
+        n = len(hi) // 2
+        calls.append([(own[j][0], own[j][1], hi[j * n:(j + 1) * n]) for j in range(len(own))])
+    off = []
+    for r in ("plane", "mate", "hop2"):
+        if sv[r] == core:
+            for X in PL["chips"]:
+                if PL["rel"](Y, X) == r:
+                    off += [(X, i) for i in range(PL["m"])]
+    h = len(lo) // 2
+    j = 0
+    while j < len(off):
+        if j + 1 < len(off):
+            calls.append([(off[j][0], off[j][1], lo[:h]), (off[j + 1][0], off[j + 1][1], lo[h:])])
+            j += 2
+        else:
+            calls.append([(off[j][0], off[j][1], lo)])
+            j += 1
+    return calls
+
+
+def rank_program(g, core, T, topo):
+    cores = list(T.cores)
+    PL = _plan(cores, topo)
+    X = topo.chip(core)
+    if X not in PL["chips"]:
+        return
+    chips, rk, m, rel = PL["chips"], PL["rk"], PL["m"], PL["rel"]
+    SL = W8 * m
+    BL = SL * m
+    rank = T.rank_of(core)
+    ktab = _table_of(core, PL, topo)
+    gate_rel = [r for r in ("mate", "hop2") if PL["gate"][X][r] == core]
+    if rank is None and ktab is None and not gate_rel:
+        return
+    V, PE, S = g.vector, g.tensor, T.sem
+    lo, hi = _engines(core, PL, topo)
+    ciX = chips.index(X)
+    sent = [0]
+    A = AluOpType
+
+    def send(trs):
+        L = []
+        for (src, dsts, eng, sem) in trs:
+            ids, aps = [], []
+            for (d, ap) in dsts:
+                assert topo.may_write(core, d) and (_mk(eng) & ~topo.mask(core, d)) == 0
+                a = topo.addr(d)
+                ids.append(DstId(rid=a[0], pnc=a[1]))
+                aps.append(ap)
+            L.append(RemoteDMATransfer(dst_ids=ids, dma_engine_mask=_mk(eng), remote_sem=sem,
+                                       srcs=[src], dsts=aps, alu_op=0))
+            sent[0] += len(eng)
+        g.remote_dma_fused(L, local_sem=S.sent)
+
+    def uniq(seq):
+        out = []
+        for c in seq:
+            if c not in out:
+                out.append(c)
+        return out
+
+    if rank is not None:
+        i_me = rk[X].index(core)
+        g.sync.dma_start(T.e_i[:, :], T.idx[:, :]).then_inc(S.s_idx, 16)
+        g.sync.dma_start(T.tabS[:, :], T.tab[:, :]).then_inc(S.s_tab, 16)
+        V.memset(T.ones_b[:, :], 1.0).then_inc(S.s_ms, 1)
+        V.memset(T.opad[:, 0:36], 0.0).then_inc(S.s_ms, 1)
+        g.iota(T.io96[:, :], [[1, 96]], 0, 0, allow_small_or_imprecise_dtypes=True).then_inc(S.cga, 1)
+        g.iota(T.rowc[:, :], [[0, 4], [CAP, 12]], 0, 0, allow_small_or_imprecise_dtypes=True).then_inc(S.cga, 1)
+        g.wait_ge(S.s_ms, 2)
+        g.affine_select(T.ut[:, :], T.ones_b[:, :], [[1, 128]], A.is_gt, 0.0, 0, -1).then_inc(S.cga, 1)
+        g.iota(T.iom16[:, :], [[0, 8], [1, 16]], 0, 0, allow_small_or_imprecise_dtypes=True).then_inc(S.cga, 1)
+        g.iota(T.p_i[:, :], [[0, 1]], 0, 1).then_inc(S.cgb, 1)
+        g.iota(T.ioc4[:, :], [[1, 8], [0, 4]], 0, 0, allow_small_or_imprecise_dtypes=True).then_inc(S.cgb, 1)
+        V.wait_ge(S.s_idx, 16)
+        V.tensor_scalar(out=T.ol_i[:, 0:4], in0=T.e_i[:, :], scalar1=12, scalar2=None,
+                        op0=A.logical_shift_right).then_inc(S.s1, 1)
+        V.tensor_scalar(out=T.ol_i[:, 4:8], in0=T.e_i[:, :], scalar1=RCOL - 1, scalar2=None,
+                        op0=A.bitwise_and).then_inc(S.s1, 1)
+        V.wait_ge(S.s1, 2)
+        V.tensor_copy(out=T.ol_f[:, :], in_=T.ol_i[:, :]).then_inc(S.s2, 1)
+        V.wait_ge(S.s2, 1)
+        V.wait_ge(S.cga, 4)
+        for c in range(4):
+            V.tensor_scalar(out=T.opad[:, 36 + 12 * c:48 + 12 * c], in0=T.io96[:, 0:12], scalar1=T.ol_f[:, c:c + 1],
+                            scalar2=None, op0=A.is_equal).then_inc(S.s3, 1)
+        PE.wait_ge(S.s_ms, 2)
+        PE.wait_ge(S.cga, 4)
+        PE.matmul(T.cnt_ps[:, 0:48], T.ones_b[0:1, :], T.rowc[0:1, :], True, False).then_inc(S.s4, 1)
+        PE.wait_ge(S.s3, 4)
+        PE.matmul(T.cnt_ps[:, 0:48], T.ut[:, :], T.opad[:, 36:84], False, False).then_inc(S.s4, 1)
+        for s in (1, 2, 3):
+            PE.matmul(T.cnt_ps[:, 0:48], T.ones_b[:, :], T.opad[:, 36 - 12 * s:84 - 12 * s], False,
+                      s == 3).then_inc(S.s4, 1)
+        V.wait_ge(S.s3, 4)
+        V.wait_ge(S.s4, 5)
+        V.tensor_tensor(out=T.tmpv[:, :], in0=T.cnt_ps[:, 0:48], in1=T.opad[:, 36:84], op=A.mult).then_inc(S.s5, 1)
+        V.wait_ge(S.s5, 1)
+        for c in range(4):
+            V.tensor_reduce(out=T.pos_f[:, c:c + 1], in_=T.tmpv[:, 12 * c:12 * c + 12], axis=AxisListType.X,
+                            op=A.add).then_inc(S.s6, 1)
+        V.wait_ge(S.s6, 4)
+        V.tensor_copy(out=T.pos_i[:, :], in_=T.pos_f[:, :]).then_inc(S.s7, 1)
+        V.wait_ge(S.s7, 1)
+        V.tensor_scalar(out=T.hl_i[:, 0:4], in0=T.pos_i[:, :], scalar1=15, scalar2=None,
+                        op0=A.bitwise_and).then_inc(S.s8, 1)
+        V.tensor_scalar(out=T.hl_i[:, 4:8], in0=T.pos_i[:, :], scalar1=4, scalar2=None,
+                        op0=A.logical_shift_right).then_inc(S.s8, 1)
+        V.wait_ge(S.s8, 2)
+        V.tensor_copy(out=T.hl_f[:, :], in_=T.hl_i[:, :]).then_inc(S.s9, 1)
+        V.wait_ge(S.s9, 1)
+        for c in range(4):
+            V.tensor_scalar(out=T.amat[:, 128 * c:128 * c + 128], in0=T.iom16[:, :], scalar1=T.hl_f[:, c:c + 1],
+                            scalar2=T.ol_f[:, 4 + c:5 + c], op0=A.is_equal, op1=A.mult).then_inc(S.s10, 1)
+            V.tensor_scalar(out=T.bmat[:, 96 * c:96 * c + 96], in0=T.io96[:, :], scalar1=T.hl_f[:, 4 + c:5 + c],
+                            scalar2=None, op0=A.is_equal).then_inc(S.s10, 1)
+        PE.wait_ge(S.s10, 8)
+        for c in range(4):
+            PE.matmul(T.rq_ps[:, 0:96], T.amat[:, 128 * c:128 * c + 128], T.bmat[:, 96 * c:96 * c + 96], c == 0,
+                      c == 3).then_inc(S.s11, 1)
+        V.wait_ge(S.s11, 4)
+        V.tensor_copy(out=T.req[:, :], in_=T.rq_ps[:, 0:96]).then_inc(S.s12, 1)
+
+        g.wait_ge(S.s12, 1)
+        h = len(hi) // 2
+        first, second = [], []
+        for Y in chips:
+            ciY = chips.index(Y)
+            src = T.req[:, ciY * SL:(ciY + 1) * SL]
+            r = rel(X, Y)
+            dcol = ciX * BL + i_me * SL
+            if r in ("mate", "hop2"):
+                eng = hi[:h] if r == "mate" else hi[h:]
+                first.append((src, [(PL["gate"][X][r], T.gw[:, i_me * SL:(i_me + 1) * SL])], eng, S.gwin))
+            elif r == "plane":
+                ds = uniq([PL["serv"][(Y, k)]["plane"] for k in range(m)])
+                second.append((src, [(d, T.rq[:, dcol:dcol + SL]) for d in ds], lo, S["rq%d" % ciX]))
+            else:
+                ds = [c for c in rk[X] if c != core]
+                second.append((src, [(d, T.rq[:, dcol:dcol + SL]) for d in ds], hi, S["rq%d" % ciX]))
+        send(first)
+        send(second)
+        g.wait_ge(S.s_tab, 16)
+        send([(T.tabS[:, :], [(PL["helper"][(X, i_me)], T.tabS[:, :])], lo + hi, S.tabin)])
+
+        V.wait_ge(S.cgb, 2)
+        V.tensor_scalar(out=T.pc_i[:, 0:1], in0=T.p_i[:, :], scalar1=7, scalar2=None,
+                        op0=A.bitwise_and).then_inc(S.k1, 1)
+        V.tensor_scalar(out=T.pc_i[:, 1:2], in0=T.p_i[:, :], scalar1=3, scalar2=None,
+                        op0=A.logical_shift_right).then_inc(S.k1, 1)
+        V.wait_ge(S.k1, 2)
+        V.tensor_copy(out=T.pc_f[:, :], in_=T.pc_i[:, :]).then_inc(S.k2, 1)
+        V.wait_ge(S.k2, 1)
+        V.tensor_scalar(out=T.mk[:, :], in0=T.ioc4[:, :], scalar1=T.pc_f[:, 0:1], scalar2=None,
+                        op0=A.is_equal).then_inc(S.k3, 1)
+        V.tensor_scalar(out=T.l2[:, :], in0=T.iom16[:, :], scalar1=T.pc_f[:, 1:2], scalar2=None,
+                        op0=A.is_equal).then_inc(S.k3, 1)
+        V.wait_ge(S.k3, 2)
+        for c in range(4):
+            V.tensor_scalar(out=T.rhs2[:, c:32:4], in0=T.mk[:, c:32:4], scalar1=T.pos_f[:, c:c + 1], scalar2=None,
+                            op0=A.mult).then_inc(S.s13, 1)
+        PE.wait_ge(S.k3, 2)
+        PE.wait_ge(S.s13, 4)
+        PE.matmul(T.po_ps[:, 0:32], T.l2[:, :], T.rhs2[:, :], True, True).then_inc(S.s14, 1)
+        V.wait_ge(S.s14, 1)
+        V.tensor_copy(out=T.posoff[:, :], in_=T.po_ps[:, 0:32]).then_inc(S.s15, 1)
+        V.wait_ge(S.s12, 1)
+        V.wait_ge(S.s_tab, 16)
+        V.tensor_copy(out=T.land[:, rank * CAP:(rank + 1) * CAP],
+                      in_=T.tabS[:, 0:RCOL].indirect(T.req[:, rank * W8:(rank + 1) * W8])).then_inc(S.selfg, 1)
+    else:
+        if ktab is not None:
+            V.wait_ge(S.tabin, len(lo) + len(hi))
+
+    for r in gate_rel:
+        g.wait_ge(S.gwin, m * (len(hi) // 2))
+        Y = [Z for Z in chips if rel(X, Z) == r][0]
+        ds = uniq([PL["serv"][(Y, k)][r] for k in range(m)])
+        send([(T.gw[:, 0:BL], [(d, T.rq[:, ciX * BL:(ciX + 1) * BL]) for d in ds], lo, S["rq%d" % ciX])])
+
+    if ktab is not None:
+        owner = ciX * m + ktab
+        waited = []
+        for n, call in enumerate(_sched(core, PL, topo)):
+            trs = []
+            for (Z, i, eng) in call:
+                ciZ = chips.index(Z)
+                if ciZ not in waited:
+                    r = rel(X, Z)
+                    tot = {"own": (m - 1) * len(hi), "plane": m * len(lo), "mate": len(lo), "hop2": len(lo)}[r]
+                    V.wait_ge(S["rq%d" % ciZ], tot)
+                    waited.append(ciZ)
+                rr = ciZ * m + i
+                col = ciZ * BL + i * SL + ktab * W8
+                V.tensor_copy(out=T.rep[:, rr * CAP:(rr + 1) * CAP],
+                              in_=T.tabS[:, 0:RCOL].indirect(T.rq[:, col:col + W8])).then_inc(S["gth%d" % n], 1)
+                trs.append((T.rep[:, rr * CAP:(rr + 1) * CAP],
+                            [(rk[Z][i], T.land[:, owner * CAP:(owner + 1) * CAP])], eng, S.got))
+            g.wait_ge(S["gth%d" % n], len(call))
+            send(trs)
+
+    if rank is not None:
+        tot = 0
+        for Z in chips:
+            for c in PL["on"][Z]:
+                for call in _sched(c, PL, topo):
+                    for (Q, i, eng) in call:
+                        if rk[Q][i] == core:
+                            tot += len(eng)
+        V.wait_ge(S.got, tot)
+        V.wait_ge(S.selfg, 1)
+        V.wait_ge(S.s15, 1)
+        V.tensor_copy(out=T.yS[:, :], in_=T.land[:, 0:12 * CAP].indirect(T.posoff[:, 0:32])).then_inc(S.fin, 1)
+        g.sync.wait_ge(S.fin, 1)
+        g.sync.dma_start(T.y[:, :], T.yS[:, :]).then_inc(S.ydone, 16)
+        g.sync.wait_ge(S.ydone, 16)
+    if sent[0]:
+        g.wait_ge(S.sent, sent[0])

@@ -5,47 +5,24 @@ RCOL = 4096
 CAP = 128
 NENT = 512
 W8 = CAP // 16
+NCH = 4
+EARLY = 3
+FSPLIT = 2
 
-SCRATCH = {
-    "tabS": ("sbuf", [128, RCOL], "bfloat16"),
-    "e_i": ("sbuf", [128, 4], "int32"),
-    "ol_i": ("sbuf", [128, 8], "int32"),
-    "ol_f": ("sbuf", [128, 8], "float32"),
-    "opad": ("sbuf", [128, 84], "bfloat16"),
-    "ones_b": ("sbuf", [128, 128], "bfloat16"),
-    "ut": ("sbuf", [128, 128], "bfloat16"),
-    "rowc": ("sbuf", [128, 48], "bfloat16"),
-    "io96": ("sbuf", [128, 96], "float32"),
-    "iom16": ("sbuf", [128, 128], "float32"),
-    "ioc4": ("sbuf", [128, 32], "float32"),
-    "p_i": ("sbuf", [128, 1], "int32"),
-    "pc_i": ("sbuf", [128, 2], "int32"),
-    "pc_f": ("sbuf", [128, 2], "float32"),
-    "mk": ("sbuf", [128, 32], "float32"),
-    "l2": ("sbuf", [128, 128], "float32"),
-    "tmpv": ("sbuf", [128, 48], "float32"),
-    "pos_f": ("sbuf", [128, 4], "float32"),
-    "pos_i": ("sbuf", [128, 4], "int32"),
-    "hl_i": ("sbuf", [128, 8], "int32"),
-    "hl_f": ("sbuf", [128, 8], "float32"),
-    "amat": ("sbuf", [128, 512], "float32"),
-    "bmat": ("sbuf", [128, 384], "float32"),
-    "req": ("sbuf", [128, 96], "uint16"),
-    "rhs2": ("sbuf", [128, 32], "float32"),
-    "posoff": ("sbuf", [128, 32], "uint16"),
-    "gw": ("sbuf", [128, 72], "uint16"),
-    "rq": ("sbuf", [128, 288], "uint16"),
-    "rep": ("sbuf", [128, 1536], "bfloat16"),
-    "land": ("sbuf", [128, 1536], "bfloat16"),
-    "yS": ("sbuf", [128, NENT], "bfloat16"),
-    "cnt_ps": ("psum", [128, 512], "float32"),
-    "rq_ps": ("psum", [128, 512], "float32"),
-    "po_ps": ("psum", [128, 512], "float32"),
-}
-SEMAPHORES = (["s_idx", "s_tab", "s_ms", "cga", "cgb", "k1", "k2", "k3"]
+_F, _B, _I, _U = "float32", "bfloat16", "int32", "uint16"
+SCRATCH = {n: ("sbuf", [128, w], d) for (n, w, d) in [
+    ("tabS", RCOL, _B), ("e_i", 4, _I), ("ol_i", 8, _I), ("ol_f", 8, _F), ("opad", 84, _B), ("ones_b", 128, _B),
+    ("ut", 128, _B), ("rowc", 48, _B), ("io96", 96, _F), ("iom16", 128, _F), ("ioc4", 32, _F), ("p_i", 1, _I),
+    ("pc_i", 2, _I), ("pc_f", 2, _F), ("mk", 32, _F), ("l2", 128, _F), ("tmpv", 48, _F), ("pos_f", 4, _F),
+    ("pos_i", 4, _I), ("hl_i", 8, _I), ("hl_f", 8, _F), ("amat", 512, _F), ("bmat", 384, _F), ("req", 96, _U),
+    ("rhs2", 32, _F), ("posoff", 32, _U), ("gw", 72, _U), ("rq", 288, _U), ("rep", 1536, _B), ("land", 1536, _B),
+    ("yS", NENT, _B)]}
+SCRATCH.update({n: ("psum", [128, 512], _F) for n in ("cnt_ps", "rq_ps", "po_ps")})
+SEMAPHORES = (["s_idx", "s_ms", "cga", "cgb", "k1", "k2", "k3"]
               + ["s%d" % i for i in range(1, 16)]
-              + ["gwin", "tabin", "rq0", "rq1", "rq2", "rq3", "got", "sent", "selfg", "fin", "ydone"]
-              + ["gth%d" % i for i in range(6)])
+              + ["gwin", "tabin", "rq0", "rq1", "rq2", "rq3", "got", "sent", "selfg"]
+              + ["gth%d" % i for i in range(6)] + ["tl%d" % i for i in range(NCH)]
+              + ["fin%d" % i for i in range(FSPLIT)] + ["yd%d" % i for i in range(FSPLIT)])
 
 
 def _bits(m):
@@ -167,6 +144,7 @@ def rank_program(g, core, T, topo):
     ciX = chips.index(X)
     sent = [0]
     A = AluOpType
+    CW = RCOL // NCH
 
     def send(trs):
         L = []
@@ -189,31 +167,47 @@ def rank_program(g, core, T, topo):
                 out.append(c)
         return out
 
+    def ts(out, in0, s1, op0, sem, s2=None, op1=None):
+        if op1 is None:
+            V.tensor_scalar(out=out, in0=in0, scalar1=s1, scalar2=None, op0=op0).then_inc(sem, 1)
+        else:
+            V.tensor_scalar(out=out, in0=in0, scalar1=s1, scalar2=s2, op0=op0, op1=op1).then_inc(sem, 1)
+
+    def cp(out, in_, sem):
+        V.tensor_copy(out=out, in_=in_).then_inc(sem, 1)
+
+    def io(out, pat, cm, sem):
+        g.iota(out, pat, 0, cm, allow_small_or_imprecise_dtypes=True).then_inc(sem, 1)
+
+    def copy_piece(ch):
+        g.wait_ge(S["tl%d" % ch], 16)
+        ap = T.tabS[:, ch * CW:(ch + 1) * CW]
+        send([(ap, [(PL["helper"][(X, rk[X].index(core))], ap)], lo + hi, S.tabin)])
+
     if rank is not None:
         i_me = rk[X].index(core)
         g.sync.dma_start(T.e_i[:, :], T.idx[:, :]).then_inc(S.s_idx, 16)
-        g.sync.dma_start(T.tabS[:, :], T.tab[:, :]).then_inc(S.s_tab, 16)
+        for ch in range(NCH):
+            g.sync.dma_start(T.tabS[:, ch * CW:(ch + 1) * CW],
+                             T.tab[:, ch * CW:(ch + 1) * CW]).then_inc(S["tl%d" % ch], 16)
         V.memset(T.ones_b[:, :], 1.0).then_inc(S.s_ms, 1)
         V.memset(T.opad[:, 0:36], 0.0).then_inc(S.s_ms, 1)
-        g.iota(T.io96[:, :], [[1, 96]], 0, 0, allow_small_or_imprecise_dtypes=True).then_inc(S.cga, 1)
-        g.iota(T.rowc[:, :], [[0, 4], [CAP, 12]], 0, 0, allow_small_or_imprecise_dtypes=True).then_inc(S.cga, 1)
+        io(T.io96[:, :], [[1, 96]], 0, S.cga)
+        io(T.rowc[:, :], [[0, 4], [CAP, 12]], 0, S.cga)
         g.wait_ge(S.s_ms, 2)
         g.affine_select(T.ut[:, :], T.ones_b[:, :], [[1, 128]], A.is_gt, 0.0, 0, -1).then_inc(S.cga, 1)
-        g.iota(T.iom16[:, :], [[0, 8], [1, 16]], 0, 0, allow_small_or_imprecise_dtypes=True).then_inc(S.cga, 1)
+        io(T.iom16[:, :], [[0, 8], [1, 16]], 0, S.cga)
         g.iota(T.p_i[:, :], [[0, 1]], 0, 1).then_inc(S.cgb, 1)
-        g.iota(T.ioc4[:, :], [[1, 8], [0, 4]], 0, 0, allow_small_or_imprecise_dtypes=True).then_inc(S.cgb, 1)
+        io(T.ioc4[:, :], [[1, 8], [0, 4]], 0, S.cgb)
         V.wait_ge(S.s_idx, 16)
-        V.tensor_scalar(out=T.ol_i[:, 0:4], in0=T.e_i[:, :], scalar1=12, scalar2=None,
-                        op0=A.logical_shift_right).then_inc(S.s1, 1)
-        V.tensor_scalar(out=T.ol_i[:, 4:8], in0=T.e_i[:, :], scalar1=RCOL - 1, scalar2=None,
-                        op0=A.bitwise_and).then_inc(S.s1, 1)
+        ts(T.ol_i[:, 0:4], T.e_i[:, :], 12, A.logical_shift_right, S.s1)
+        ts(T.ol_i[:, 4:8], T.e_i[:, :], RCOL - 1, A.bitwise_and, S.s1)
         V.wait_ge(S.s1, 2)
-        V.tensor_copy(out=T.ol_f[:, :], in_=T.ol_i[:, :]).then_inc(S.s2, 1)
+        cp(T.ol_f[:, :], T.ol_i[:, :], S.s2)
         V.wait_ge(S.s2, 1)
         V.wait_ge(S.cga, 4)
         for c in range(4):
-            V.tensor_scalar(out=T.opad[:, 36 + 12 * c:48 + 12 * c], in0=T.io96[:, 0:12], scalar1=T.ol_f[:, c:c + 1],
-                            scalar2=None, op0=A.is_equal).then_inc(S.s3, 1)
+            ts(T.opad[:, 36 + 12 * c:48 + 12 * c], T.io96[:, 0:12], T.ol_f[:, c:c + 1], A.is_equal, S.s3)
         PE.wait_ge(S.s_ms, 2)
         PE.wait_ge(S.cga, 4)
         PE.matmul(T.cnt_ps[:, 0:48], T.ones_b[0:1, :], T.rowc[0:1, :], True, False).then_inc(S.s4, 1)
@@ -230,27 +224,26 @@ def rank_program(g, core, T, topo):
             V.tensor_reduce(out=T.pos_f[:, c:c + 1], in_=T.tmpv[:, 12 * c:12 * c + 12], axis=AxisListType.X,
                             op=A.add).then_inc(S.s6, 1)
         V.wait_ge(S.s6, 4)
-        V.tensor_copy(out=T.pos_i[:, :], in_=T.pos_f[:, :]).then_inc(S.s7, 1)
+        cp(T.pos_i[:, :], T.pos_f[:, :], S.s7)
         V.wait_ge(S.s7, 1)
-        V.tensor_scalar(out=T.hl_i[:, 0:4], in0=T.pos_i[:, :], scalar1=15, scalar2=None,
-                        op0=A.bitwise_and).then_inc(S.s8, 1)
-        V.tensor_scalar(out=T.hl_i[:, 4:8], in0=T.pos_i[:, :], scalar1=4, scalar2=None,
-                        op0=A.logical_shift_right).then_inc(S.s8, 1)
+        ts(T.hl_i[:, 0:4], T.pos_i[:, :], 15, A.bitwise_and, S.s8)
+        ts(T.hl_i[:, 4:8], T.pos_i[:, :], 4, A.logical_shift_right, S.s8)
         V.wait_ge(S.s8, 2)
-        V.tensor_copy(out=T.hl_f[:, :], in_=T.hl_i[:, :]).then_inc(S.s9, 1)
+        cp(T.hl_f[:, :], T.hl_i[:, :], S.s9)
         V.wait_ge(S.s9, 1)
         for c in range(4):
-            V.tensor_scalar(out=T.amat[:, 128 * c:128 * c + 128], in0=T.iom16[:, :], scalar1=T.hl_f[:, c:c + 1],
-                            scalar2=T.ol_f[:, 4 + c:5 + c], op0=A.is_equal, op1=A.mult).then_inc(S.s10, 1)
-            V.tensor_scalar(out=T.bmat[:, 96 * c:96 * c + 96], in0=T.io96[:, :], scalar1=T.hl_f[:, 4 + c:5 + c],
-                            scalar2=None, op0=A.is_equal).then_inc(S.s10, 1)
+            ts(T.amat[:, 128 * c:128 * c + 128], T.iom16[:, :], T.hl_f[:, c:c + 1], A.is_equal, S.s10,
+               T.ol_f[:, 4 + c:5 + c], A.mult)
+            ts(T.bmat[:, 96 * c:96 * c + 96], T.io96[:, :], T.hl_f[:, 4 + c:5 + c], A.is_equal, S.s10)
         PE.wait_ge(S.s10, 8)
         for c in range(4):
             PE.matmul(T.rq_ps[:, 0:96], T.amat[:, 128 * c:128 * c + 128], T.bmat[:, 96 * c:96 * c + 96], c == 0,
                       c == 3).then_inc(S.s11, 1)
         V.wait_ge(S.s11, 4)
-        V.tensor_copy(out=T.req[:, :], in_=T.rq_ps[:, 0:96]).then_inc(S.s12, 1)
+        cp(T.req[:, :], T.rq_ps[:, 0:96], S.s12)
 
+        for ch in range(EARLY):
+            copy_piece(ch)
         g.wait_ge(S.s12, 1)
         h = len(hi) // 2
         first, second = [], []
@@ -270,37 +263,32 @@ def rank_program(g, core, T, topo):
                 second.append((src, [(d, T.rq[:, dcol:dcol + SL]) for d in ds], hi, S["rq%d" % ciX]))
         send(first)
         send(second)
-        g.wait_ge(S.s_tab, 16)
-        send([(T.tabS[:, :], [(PL["helper"][(X, i_me)], T.tabS[:, :])], lo + hi, S.tabin)])
+        for ch in range(EARLY, NCH):
+            copy_piece(ch)
 
         V.wait_ge(S.cgb, 2)
-        V.tensor_scalar(out=T.pc_i[:, 0:1], in0=T.p_i[:, :], scalar1=7, scalar2=None,
-                        op0=A.bitwise_and).then_inc(S.k1, 1)
-        V.tensor_scalar(out=T.pc_i[:, 1:2], in0=T.p_i[:, :], scalar1=3, scalar2=None,
-                        op0=A.logical_shift_right).then_inc(S.k1, 1)
+        ts(T.pc_i[:, 0:1], T.p_i[:, :], 7, A.bitwise_and, S.k1)
+        ts(T.pc_i[:, 1:2], T.p_i[:, :], 3, A.logical_shift_right, S.k1)
         V.wait_ge(S.k1, 2)
-        V.tensor_copy(out=T.pc_f[:, :], in_=T.pc_i[:, :]).then_inc(S.k2, 1)
+        cp(T.pc_f[:, :], T.pc_i[:, :], S.k2)
         V.wait_ge(S.k2, 1)
-        V.tensor_scalar(out=T.mk[:, :], in0=T.ioc4[:, :], scalar1=T.pc_f[:, 0:1], scalar2=None,
-                        op0=A.is_equal).then_inc(S.k3, 1)
-        V.tensor_scalar(out=T.l2[:, :], in0=T.iom16[:, :], scalar1=T.pc_f[:, 1:2], scalar2=None,
-                        op0=A.is_equal).then_inc(S.k3, 1)
+        ts(T.mk[:, :], T.ioc4[:, :], T.pc_f[:, 0:1], A.is_equal, S.k3)
+        ts(T.l2[:, :], T.iom16[:, :], T.pc_f[:, 1:2], A.is_equal, S.k3)
         V.wait_ge(S.k3, 2)
         for c in range(4):
-            V.tensor_scalar(out=T.rhs2[:, c:32:4], in0=T.mk[:, c:32:4], scalar1=T.pos_f[:, c:c + 1], scalar2=None,
-                            op0=A.mult).then_inc(S.s13, 1)
+            ts(T.rhs2[:, c:32:4], T.mk[:, c:32:4], T.pos_f[:, c:c + 1], A.mult, S.s13)
         PE.wait_ge(S.k3, 2)
         PE.wait_ge(S.s13, 4)
         PE.matmul(T.po_ps[:, 0:32], T.l2[:, :], T.rhs2[:, :], True, True).then_inc(S.s14, 1)
         V.wait_ge(S.s14, 1)
-        V.tensor_copy(out=T.posoff[:, :], in_=T.po_ps[:, 0:32]).then_inc(S.s15, 1)
+        cp(T.posoff[:, :], T.po_ps[:, 0:32], S.s15)
         V.wait_ge(S.s12, 1)
-        V.wait_ge(S.s_tab, 16)
-        V.tensor_copy(out=T.land[:, rank * CAP:(rank + 1) * CAP],
-                      in_=T.tabS[:, 0:RCOL].indirect(T.req[:, rank * W8:(rank + 1) * W8])).then_inc(S.selfg, 1)
-    else:
-        if ktab is not None:
-            V.wait_ge(S.tabin, len(lo) + len(hi))
+        for ch in range(NCH):
+            V.wait_ge(S["tl%d" % ch], 16)
+        cp(T.land[:, rank * CAP:(rank + 1) * CAP],
+           T.tabS[:, 0:RCOL].indirect(T.req[:, rank * W8:(rank + 1) * W8]), S.selfg)
+    elif ktab is not None:
+        V.wait_ge(S.tabin, NCH * (len(lo) + len(hi)))
 
     for r in gate_rel:
         g.wait_ge(S.gwin, m * (len(hi) // 2))
@@ -322,8 +310,8 @@ def rank_program(g, core, T, topo):
                     waited.append(ciZ)
                 rr = ciZ * m + i
                 col = ciZ * BL + i * SL + ktab * W8
-                V.tensor_copy(out=T.rep[:, rr * CAP:(rr + 1) * CAP],
-                              in_=T.tabS[:, 0:RCOL].indirect(T.rq[:, col:col + W8])).then_inc(S["gth%d" % n], 1)
+                cp(T.rep[:, rr * CAP:(rr + 1) * CAP], T.tabS[:, 0:RCOL].indirect(T.rq[:, col:col + W8]),
+                   S["gth%d" % n])
                 trs.append((T.rep[:, rr * CAP:(rr + 1) * CAP],
                             [(rk[Z][i], T.land[:, owner * CAP:(owner + 1) * CAP])], eng, S.got))
             g.wait_ge(S["gth%d" % n], len(call))
@@ -340,9 +328,13 @@ def rank_program(g, core, T, topo):
         V.wait_ge(S.got, tot)
         V.wait_ge(S.selfg, 1)
         V.wait_ge(S.s15, 1)
-        V.tensor_copy(out=T.yS[:, :], in_=T.land[:, 0:12 * CAP].indirect(T.posoff[:, 0:32])).then_inc(S.fin, 1)
-        g.sync.wait_ge(S.fin, 1)
-        g.sync.dma_start(T.y[:, :], T.yS[:, :]).then_inc(S.ydone, 16)
-        g.sync.wait_ge(S.ydone, 16)
+        FW = NENT // FSPLIT
+        for f in range(FSPLIT):
+            q = g.sync if f % 2 == 0 else g.scalar
+            cp(T.yS[:, f * FW:(f + 1) * FW],
+               T.land[:, 0:12 * CAP].indirect(T.posoff[:, f * FW // 16:(f + 1) * FW // 16]), S["fin%d" % f])
+            q.wait_ge(S["fin%d" % f], 1)
+            q.dma_start(T.y[:, f * FW:(f + 1) * FW], T.yS[:, f * FW:(f + 1) * FW]).then_inc(S["yd%d" % f], 16)
+            q.wait_ge(S["yd%d" % f], 16)
     if sent[0]:
         g.wait_ge(S.sent, sent[0])

@@ -1,26 +1,26 @@
 from concourse.bass import DstId, RemoteDMATransfer
-from concourse.mybir import AluOpType, AxisListType
+from concourse.mybir import AluOpType, AxisListType, ActivationFunctionType
 
 RCOL = 4096
 CAP = 128
 NENT = 512
 W8 = CAP // 16
-NCH = 4
-EARLY = 3
+PIECES = [(0, 1024), (1024, 2048), (2048, 3072), (3072, RCOL)]
 FSPLIT = 2
+NCH = len(PIECES)
 
 _F, _B, _I, _U = "float32", "bfloat16", "int32", "uint16"
 SCRATCH = {n: ("sbuf", [128, w], d) for (n, w, d) in [
-    ("tabS", RCOL, _B), ("e_i", 4, _I), ("ol_i", 8, _I), ("ol_f", 8, _F), ("opad", 84, _B), ("ones_b", 128, _B),
-    ("ut", 128, _B), ("rowc", 48, _B), ("io96", 96, _F), ("iom16", 128, _F), ("ioc4", 32, _F), ("p_i", 1, _I),
+    ("tabS", RCOL, _B), ("e_i", 4, _I), ("ol_i", 12, _I), ("ol_f", 12, _F), ("opad", 84, _B), ("ones_b", 128, _B),
+    ("ut", 128, _B), ("rowc", 48, _B), ("io96", 96, _B), ("iom16", 128, _B), ("ioc4", 32, _F), ("p_i", 1, _I),
     ("pc_i", 2, _I), ("pc_f", 2, _F), ("mk", 32, _F), ("l2", 128, _F), ("tmpv", 48, _F), ("pos_f", 4, _F),
-    ("pos_i", 4, _I), ("hl_i", 8, _I), ("hl_f", 8, _F), ("amat", 512, _F), ("bmat", 384, _F), ("req", 96, _U),
-    ("rhs2", 32, _F), ("posoff", 32, _U), ("gw", 72, _U), ("rq", 288, _U), ("rep", 1536, _B), ("land", 1536, _B),
-    ("yS", NENT, _B)]}
+    ("pos_i", 4, _I), ("hl_i", 8, _I), ("hl_f", 8, _F), ("amat", 1024, _B), ("bmat", 384, _B), ("req", 96, _U),
+    ("rhs2", 32, _F), ("posoff", 32, _U), ("gw", 72, _U), ("gwf", 72, _U), ("rq", 288, _U), ("rep", 1536, _B),
+    ("land", 1536, _B), ("yS", NENT, _B)]}
 SCRATCH.update({n: ("psum", [128, 512], _F) for n in ("cnt_ps", "rq_ps", "po_ps")})
-SEMAPHORES = (["s_idx", "s_ms", "cga", "cgb", "k1", "k2", "k3"]
+SEMAPHORES = (["s_idx", "s_ms", "cga", "cgb", "k1", "k2", "k3", "sl1", "sl2", "ab0", "ab1", "ab2", "ab3"]
               + ["s%d" % i for i in range(1, 16)]
-              + ["gwin", "tabin", "rq0", "rq1", "rq2", "rq3", "got", "sent", "selfg"]
+              + ["gwin", "gwfin", "gwl", "tabin", "rq0", "rq1", "rq2", "rq3", "got", "sent", "selfg"]
               + ["gth%d" % i for i in range(6)] + ["tl%d" % i for i in range(NCH)]
               + ["fin%d" % i for i in range(FSPLIT)] + ["yd%d" % i for i in range(FSPLIT)])
 
@@ -56,7 +56,7 @@ def _plan(cores, topo):
             return "plane"
         return "hop2"
 
-    serv, helper, gate = {}, {}, {}
+    serv, helper, gslow, gfast = {}, {}, {}, {}
     for X in chips:
         far = rk[[Y for Y in chips if topo.mates(X, Y)][0]][0]
         ports = [c for c in on[X] if topo.may_write(c, far)]
@@ -72,10 +72,11 @@ def _plan(cores, topo):
                 serv[(X, k)] = {"own": c, "plane": c, "mate": h, "hop2": h}
             used.append(h)
             helper[(X, k)] = h
-        gs = [helper[(X, k)] for k in range(m) if helper[(X, k)] in ports]
-        assert len(gs) >= 2
-        gate[X] = {"mate": gs[0], "hop2": gs[1]}
-    return {"chips": chips, "on": on, "rk": rk, "m": m, "rel": rel, "serv": serv, "helper": helper, "gate": gate}
+        gslow[X] = [helper[(X, k)] for k in range(m) if helper[(X, k)] in ports]
+        gfast[X] = [c for c in rk[X] if c in ports][0]
+        assert len(gslow[X]) >= 1
+    return {"chips": chips, "on": on, "rk": rk, "m": m, "rel": rel, "serv": serv, "helper": helper,
+            "gslow": gslow, "gfast": gfast}
 
 
 def _engines(core, PL, topo):
@@ -107,21 +108,19 @@ def _sched(core, PL, topo):
         own = [(Y, i) for i in range(PL["m"]) if i != k]
         n = len(hi) // 2
         calls.append([(own[j][0], own[j][1], hi[j * n:(j + 1) * n]) for j in range(len(own))])
-    off = []
-    for r in ("plane", "mate", "hop2"):
-        if sv[r] == core:
-            for X in PL["chips"]:
-                if PL["rel"](Y, X) == r:
-                    off += [(X, i) for i in range(PL["m"])]
     h = len(lo) // 2
-    j = 0
-    while j < len(off):
-        if j + 1 < len(off):
-            calls.append([(off[j][0], off[j][1], lo[:h]), (off[j + 1][0], off[j + 1][1], lo[h:])])
-            j += 2
-        else:
-            calls.append([(off[j][0], off[j][1], lo)])
-            j += 1
+    for r in ("plane", "hop2", "mate"):
+        if sv[r] != core:
+            continue
+        off = [(X, i) for X in PL["chips"] if PL["rel"](Y, X) == r for i in range(PL["m"])]
+        j = 0
+        while j < len(off):
+            if j + 1 < len(off):
+                calls.append([(off[j][0], off[j][1], lo[:h]), (off[j + 1][0], off[j + 1][1], lo[h:])])
+                j += 2
+            else:
+                calls.append([(off[j][0], off[j][1], lo)])
+                j += 1
     return calls
 
 
@@ -136,15 +135,14 @@ def rank_program(g, core, T, topo):
     BL = SL * m
     rank = T.rank_of(core)
     ktab = _table_of(core, PL, topo)
-    gate_rel = [r for r in ("mate", "hop2") if PL["gate"][X][r] == core]
-    if rank is None and ktab is None and not gate_rel:
+    if rank is None and ktab is None:
         return
-    V, PE, S = g.vector, g.tensor, T.sem
+    V, PE, S, AC = g.vector, g.tensor, T.sem, g.scalar
     lo, hi = _engines(core, PL, topo)
+    gslow, gfast = PL["gslow"][X], PL["gfast"][X]
     ciX = chips.index(X)
     sent = [0]
     A = AluOpType
-    CW = RCOL // NCH
 
     def send(trs):
         L = []
@@ -176,20 +174,25 @@ def rank_program(g, core, T, topo):
     def cp(out, in_, sem):
         V.tensor_copy(out=out, in_=in_).then_inc(sem, 1)
 
+    def gather(q, out, in_, sem):
+        if q is V:
+            V.tensor_copy(out=out, in_=in_).then_inc(sem, 1)
+        else:
+            AC.activation(out=out, in_=in_, func=ActivationFunctionType.Copy, bias=-0.0, scale=1.0).then_inc(sem, 1)
+
     def io(out, pat, cm, sem):
         g.iota(out, pat, 0, cm, allow_small_or_imprecise_dtypes=True).then_inc(sem, 1)
 
-    def copy_piece(ch):
-        g.wait_ge(S["tl%d" % ch], 16)
-        ap = T.tabS[:, ch * CW:(ch + 1) * CW]
-        send([(ap, [(PL["helper"][(X, rk[X].index(core))], ap)], lo + hi, S.tabin)])
+    def pass_on(buf, r, part, of):
+        Y = [Z for Z in chips if rel(X, Z) == r][0]
+        ds = uniq([PL["serv"][(Y, k)][r] for k in range(m)])[part::of]
+        send([(buf[:, 0:BL], [(d, T.rq[:, ciX * BL:(ciX + 1) * BL]) for d in ds], lo, S["rq%d" % ciX])])
 
     if rank is not None:
         i_me = rk[X].index(core)
         g.sync.dma_start(T.e_i[:, :], T.idx[:, :]).then_inc(S.s_idx, 16)
-        for ch in range(NCH):
-            g.sync.dma_start(T.tabS[:, ch * CW:(ch + 1) * CW],
-                             T.tab[:, ch * CW:(ch + 1) * CW]).then_inc(S["tl%d" % ch], 16)
+        for ch, (a, b) in enumerate(PIECES):
+            g.sync.dma_start(T.tabS[:, a:b], T.tab[:, a:b]).then_inc(S["tl%d" % ch], 16)
         V.memset(T.ones_b[:, :], 1.0).then_inc(S.s_ms, 1)
         V.memset(T.opad[:, 0:36], 0.0).then_inc(S.s_ms, 1)
         io(T.io96[:, :], [[1, 96]], 0, S.cga)
@@ -201,9 +204,8 @@ def rank_program(g, core, T, topo):
         io(T.ioc4[:, :], [[1, 8], [0, 4]], 0, S.cgb)
         V.wait_ge(S.s_idx, 16)
         ts(T.ol_i[:, 0:4], T.e_i[:, :], 12, A.logical_shift_right, S.s1)
-        ts(T.ol_i[:, 4:8], T.e_i[:, :], RCOL - 1, A.bitwise_and, S.s1)
-        V.wait_ge(S.s1, 2)
-        cp(T.ol_f[:, :], T.ol_i[:, :], S.s2)
+        V.wait_ge(S.s1, 1)
+        cp(T.ol_f[:, 0:4], T.ol_i[:, 0:4], S.s2)
         V.wait_ge(S.s2, 1)
         V.wait_ge(S.cga, 4)
         for c in range(4):
@@ -216,6 +218,11 @@ def rank_program(g, core, T, topo):
         for s in (1, 2, 3):
             PE.matmul(T.cnt_ps[:, 0:48], T.ones_b[:, :], T.opad[:, 36 - 12 * s:84 - 12 * s], False,
                       s == 3).then_inc(S.s4, 1)
+        ts(T.ol_i[:, 4:8], T.e_i[:, :], RCOL - 64, A.bitwise_and, S.sl1)
+        ts(T.ol_i[:, 8:12], T.e_i[:, :], 63, A.bitwise_and, S.sl1)
+        V.wait_ge(S.sl1, 2)
+        cp(T.ol_f[:, 4:12], T.ol_i[:, 4:12], S.sl2)
+        V.wait_ge(S.sl2, 1)
         V.wait_ge(S.s3, 4)
         V.wait_ge(S.s4, 5)
         V.tensor_tensor(out=T.tmpv[:, :], in0=T.cnt_ps[:, 0:48], in1=T.opad[:, 36:84], op=A.mult).then_inc(S.s5, 1)
@@ -232,29 +239,37 @@ def rank_program(g, core, T, topo):
         cp(T.hl_f[:, :], T.hl_i[:, :], S.s9)
         V.wait_ge(S.s9, 1)
         for c in range(4):
-            ts(T.amat[:, 128 * c:128 * c + 128], T.iom16[:, :], T.hl_f[:, c:c + 1], A.is_equal, S.s10,
-               T.ol_f[:, 4 + c:5 + c], A.mult)
-            ts(T.bmat[:, 96 * c:96 * c + 96], T.io96[:, :], T.hl_f[:, 4 + c:5 + c], A.is_equal, S.s10)
-        PE.wait_ge(S.s10, 8)
-        for c in range(4):
-            PE.matmul(T.rq_ps[:, 0:96], T.amat[:, 128 * c:128 * c + 128], T.bmat[:, 96 * c:96 * c + 96], c == 0,
-                      c == 3).then_inc(S.s11, 1)
-        V.wait_ge(S.s11, 4)
+            sab = S["ab%d" % c]
+            ah, al = T.amat[:, 256 * c:256 * c + 128], T.amat[:, 256 * c + 128:256 * c + 256]
+            bm = T.bmat[:, 96 * c:96 * c + 96]
+            ts(ah, T.iom16[:, :], T.hl_f[:, c:c + 1], A.is_equal, sab, T.ol_f[:, 4 + c:5 + c], A.mult)
+            ts(al, T.iom16[:, :], T.hl_f[:, c:c + 1], A.is_equal, sab, T.ol_f[:, 8 + c:9 + c], A.mult)
+            ts(bm, T.io96[:, :], T.hl_f[:, 4 + c:5 + c], A.is_equal, sab)
+            PE.wait_ge(sab, 3)
+            PE.matmul(T.rq_ps[:, 0:96], ah, bm, c == 0, False).then_inc(S.s11, 1)
+            PE.matmul(T.rq_ps[:, 0:96], al, bm, False, c == 3).then_inc(S.s11, 1)
+        V.wait_ge(S.s11, 8)
         cp(T.req[:, :], T.rq_ps[:, 0:96], S.s12)
+        V.wait_ge(S.s12, 1)
 
-        for ch in range(EARLY):
-            copy_piece(ch)
+        for ch, (a, b) in enumerate(PIECES):
+            g.wait_ge(S["tl%d" % ch], 16)
+            send([(T.tabS[:, a:b], [(PL["helper"][(X, i_me)], T.tabS[:, a:b])], lo + hi, S.tabin)])
         g.wait_ge(S.s12, 1)
-        h = len(hi) // 2
         first, second = [], []
+        mine = slice(i_me * SL, (i_me + 1) * SL)
         for Y in chips:
             ciY = chips.index(Y)
             src = T.req[:, ciY * SL:(ciY + 1) * SL]
             r = rel(X, Y)
             dcol = ciX * BL + i_me * SL
-            if r in ("mate", "hop2"):
-                eng = hi[:h] if r == "mate" else hi[h:]
-                first.append((src, [(PL["gate"][X][r], T.gw[:, i_me * SL:(i_me + 1) * SL])], eng, S.gwin))
+            if r == "mate":
+                first.append((src, [(d, T.gw[:, mine]) for d in gslow], lo, S.gwin))
+            elif r == "hop2":
+                if core == gfast:
+                    cp(T.gwf[:, mine], src, S.gwl)
+                else:
+                    first.append((src, [(gfast, T.gwf[:, mine])], hi, S.gwfin))
             elif r == "plane":
                 ds = uniq([PL["serv"][(Y, k)]["plane"] for k in range(m)])
                 second.append((src, [(d, T.rq[:, dcol:dcol + SL]) for d in ds], lo, S["rq%d" % ciX]))
@@ -263,8 +278,10 @@ def rank_program(g, core, T, topo):
                 second.append((src, [(d, T.rq[:, dcol:dcol + SL]) for d in ds], hi, S["rq%d" % ciX]))
         send(first)
         send(second)
-        for ch in range(EARLY, NCH):
-            copy_piece(ch)
+        if core == gfast:
+            g.wait_ge(S.gwfin, (m - 1) * len(hi))
+            g.wait_ge(S.gwl, 1)
+            pass_on(T.gwf, "hop2", 0, 1)
 
         V.wait_ge(S.cgb, 2)
         ts(T.pc_i[:, 0:1], T.p_i[:, :], 7, A.bitwise_and, S.k1)
@@ -282,40 +299,41 @@ def rank_program(g, core, T, topo):
         PE.matmul(T.po_ps[:, 0:32], T.l2[:, :], T.rhs2[:, :], True, True).then_inc(S.s14, 1)
         V.wait_ge(S.s14, 1)
         cp(T.posoff[:, :], T.po_ps[:, 0:32], S.s15)
-        V.wait_ge(S.s12, 1)
-        for ch in range(NCH):
-            V.wait_ge(S["tl%d" % ch], 16)
+        for q in (V, AC):
+            for ch in range(NCH):
+                q.wait_ge(S["tl%d" % ch], 16)
         cp(T.land[:, rank * CAP:(rank + 1) * CAP],
            T.tabS[:, 0:RCOL].indirect(T.req[:, rank * W8:(rank + 1) * W8]), S.selfg)
-    elif ktab is not None:
-        V.wait_ge(S.tabin, NCH * (len(lo) + len(hi)))
+    else:
+        for q in (V, AC):
+            q.wait_ge(S.tabin, NCH * (len(lo) + len(hi)))
 
-    for r in gate_rel:
-        g.wait_ge(S.gwin, m * (len(hi) // 2))
-        Y = [Z for Z in chips if rel(X, Z) == r][0]
-        ds = uniq([PL["serv"][(Y, k)][r] for k in range(m)])
-        send([(T.gw[:, 0:BL], [(d, T.rq[:, ciX * BL:(ciX + 1) * BL]) for d in ds], lo, S["rq%d" % ciX])])
+    if core in gslow:
+        g.wait_ge(S.gwin, m * len(lo))
+        pass_on(T.gw, "mate", gslow.index(core), len(gslow))
 
-    if ktab is not None:
-        owner = ciX * m + ktab
-        waited = []
-        for n, call in enumerate(_sched(core, PL, topo)):
-            trs = []
-            for (Z, i, eng) in call:
-                ciZ = chips.index(Z)
-                if ciZ not in waited:
-                    r = rel(X, Z)
-                    tot = {"own": (m - 1) * len(hi), "plane": m * len(lo), "mate": len(lo), "hop2": len(lo)}[r]
-                    V.wait_ge(S["rq%d" % ciZ], tot)
-                    waited.append(ciZ)
-                rr = ciZ * m + i
-                col = ciZ * BL + i * SL + ktab * W8
-                cp(T.rep[:, rr * CAP:(rr + 1) * CAP], T.tabS[:, 0:RCOL].indirect(T.rq[:, col:col + W8]),
+    owner = ciX * m + ktab
+    waited = {0: [], 1: []}
+    nb = 0
+    for n, call in enumerate(_sched(core, PL, topo)):
+        trs = []
+        for (Z, i, eng) in call:
+            ciZ = chips.index(Z)
+            q = (V, AC)[nb % 2]
+            if ciZ not in waited[nb % 2]:
+                r = rel(X, Z)
+                tot = {"own": (m - 1) * len(hi), "plane": m * len(lo), "mate": len(lo), "hop2": len(lo)}[r]
+                q.wait_ge(S["rq%d" % ciZ], tot)
+                waited[nb % 2].append(ciZ)
+            rr = ciZ * m + i
+            col = ciZ * BL + i * SL + ktab * W8
+            gather(q, T.rep[:, rr * CAP:(rr + 1) * CAP], T.tabS[:, 0:RCOL].indirect(T.rq[:, col:col + W8]),
                    S["gth%d" % n])
-                trs.append((T.rep[:, rr * CAP:(rr + 1) * CAP],
-                            [(rk[Z][i], T.land[:, owner * CAP:(owner + 1) * CAP])], eng, S.got))
-            g.wait_ge(S["gth%d" % n], len(call))
-            send(trs)
+            nb += 1
+            trs.append((T.rep[:, rr * CAP:(rr + 1) * CAP],
+                        [(rk[Z][i], T.land[:, owner * CAP:(owner + 1) * CAP])], eng, S.got))
+        g.wait_ge(S["gth%d" % n], len(call))
+        send(trs)
 
     if rank is not None:
         tot = 0
@@ -325,16 +343,16 @@ def rank_program(g, core, T, topo):
                     for (Q, i, eng) in call:
                         if rk[Q][i] == core:
                             tot += len(eng)
-        V.wait_ge(S.got, tot)
-        V.wait_ge(S.selfg, 1)
-        V.wait_ge(S.s15, 1)
         FW = NENT // FSPLIT
         for f in range(FSPLIT):
-            q = g.sync if f % 2 == 0 else g.scalar
-            cp(T.yS[:, f * FW:(f + 1) * FW],
-               T.land[:, 0:12 * CAP].indirect(T.posoff[:, f * FW // 16:(f + 1) * FW // 16]), S["fin%d" % f])
-            q.wait_ge(S["fin%d" % f], 1)
-            q.dma_start(T.y[:, f * FW:(f + 1) * FW], T.yS[:, f * FW:(f + 1) * FW]).then_inc(S["yd%d" % f], 16)
-            q.wait_ge(S["yd%d" % f], 16)
+            q, d = ((V, g.sync), (AC, g.scalar))[f % 2]
+            q.wait_ge(S.got, tot)
+            q.wait_ge(S.selfg, 1)
+            q.wait_ge(S.s15, 1)
+            gather(q, T.yS[:, f * FW:(f + 1) * FW],
+                   T.land[:, 0:12 * CAP].indirect(T.posoff[:, f * FW // 16:(f + 1) * FW // 16]), S["fin%d" % f])
+            d.wait_ge(S["fin%d" % f], 1)
+            d.dma_start(T.y[:, f * FW:(f + 1) * FW], T.yS[:, f * FW:(f + 1) * FW]).then_inc(S["yd%d" % f], 16)
+            d.wait_ge(S["yd%d" % f], 16)
     if sent[0]:
         g.wait_ge(S.sent, sent[0])

@@ -1,5 +1,5 @@
 from concourse.bass import DstId, RemoteDMATransfer
-from concourse.mybir import AluOpType, AxisListType, ActivationFunctionType
+from concourse.mybir import AluOpType, ActivationFunctionType
 
 RCOL = 4096
 CAP = 128
@@ -9,16 +9,17 @@ PIECES = [(0, 1024), (1024, 2048), (2048, 3072), (3072, RCOL)]
 FSPLIT = 2
 NCH = len(PIECES)
 
-_F, _B, _I, _U = "float32", "bfloat16", "int32", "uint16"
+_F, _B, _I, _U, _H = "float32", "bfloat16", "int32", "uint16", "float16"
 SCRATCH = {n: ("sbuf", [128, w], d) for (n, w, d) in [
-    ("tabS", RCOL, _B), ("e_i", 4, _I), ("ol_i", 12, _I), ("ol_f", 12, _F), ("opad", 84, _B), ("ones_b", 128, _B),
-    ("ut", 128, _B), ("rowc", 48, _B), ("io96", 96, _B), ("iom16", 128, _B), ("ioc4", 32, _F), ("p_i", 1, _I),
-    ("pc_i", 2, _I), ("pc_f", 2, _F), ("mk", 32, _F), ("l2", 128, _F), ("tmpv", 48, _F), ("pos_f", 4, _F),
-    ("pos_i", 4, _I), ("hl_i", 8, _I), ("hl_f", 8, _F), ("amat", 1024, _B), ("bmat", 384, _B), ("req", 96, _U),
-    ("rhs2", 32, _F), ("posoff", 32, _U), ("gw", 72, _U), ("gwf", 72, _U), ("rq", 288, _U), ("rep", 1536, _B),
-    ("land", 1536, _B), ("yS", NENT, _B)]}
+    ("tabS", RCOL, _B), ("e_i", 4, _I), ("ol_i", 8, _I), ("ol_f", 8, _F), ("opad", 84, _B), ("ones_b", 128, _B),
+    ("ut", 128, _B), ("rowc", 48, _B), ("io128", 128, _B), ("iom16", 128, _B), ("ioc4", 32, _F), ("p_i", 1, _I),
+    ("p_f", 1, _F), ("pc_i", 2, _I), ("pc_f", 2, _F), ("mk", 32, _F), ("l2", 128, _F), ("tmpv", 48, _F),
+    ("keep", 48, _F), ("scn", 48, _F), ("pos_i", 4, _I), ("hl_i", 8, _I), ("hl_f", 8, _F), ("amat", 512, _H),
+    ("bmat", 384, _H), ("req", 96, _U), ("rhs2", 32, _F), ("posoff", 32, _U), ("gw", 72, _U), ("gwf", 72, _U),
+    ("rq", 288, _U), ("rep", 1536, _B), ("land", 1536, _B), ("yS", NENT, _B)]}
 SCRATCH.update({n: ("psum", [128, 512], _F) for n in ("cnt_ps", "rq_ps", "po_ps")})
-SEMAPHORES = (["s_idx", "s_ms", "cga", "cgb", "k1", "k2", "k3", "sl1", "sl2", "ab0", "ab1", "ab2", "ab3"]
+SEMAPHORES = (["s_idx", "s_ms", "s_k", "c1", "c2", "c3", "c4", "c5", "s_pf", "s_ut", "k1", "k2", "k3", "sl1", "sl2",
+               "ab0", "ab1", "ab2", "ab3"]
               + ["s%d" % i for i in range(1, 16)]
               + ["gwin", "gwfin", "gwl", "tabin", "rq0", "rq1", "rq2", "rq3", "got", "sent", "selfg"]
               + ["gth%d" % i for i in range(6)] + ["tl%d" % i for i in range(NCH)]
@@ -63,18 +64,17 @@ def _plan(cores, topo):
         used = []
         for k in sorted(range(m), key=lambda k: rk[X][k] in ports):
             c = rk[X][k]
-            free = [h for h in on[X] if h not in rk[X] and h not in used]
+            free = [h for h in ports if h not in rk[X] and h not in used]
             if c in ports:
-                h = sorted(free, key=lambda h: (topo.die(h) != topo.die(c), h in ports, h))[0]
-                serv[(X, k)] = {"own": c, "plane": h, "mate": c, "hop2": c}
+                h = sorted(free, key=lambda h: (topo.die(h) == topo.die(c), h))[0]
+                serv[(X, k)] = {"own": c, "plane": c, "mate": c, "hop2": h}
             else:
-                h = sorted([h for h in free if h in ports], key=lambda h: (topo.die(h) != topo.die(c), h))[0]
+                h = sorted(free, key=lambda h: (topo.die(h) != topo.die(c), h))[0]
                 serv[(X, k)] = {"own": c, "plane": c, "mate": h, "hop2": h}
             used.append(h)
             helper[(X, k)] = h
-        gslow[X] = [helper[(X, k)] for k in range(m) if helper[(X, k)] in ports]
+        gslow[X] = [helper[(X, k)] for k in range(m)]
         gfast[X] = [c for c in rk[X] if c in ports][0]
-        assert len(gslow[X]) >= 1
     return {"chips": chips, "on": on, "rk": rk, "m": m, "rel": rel, "serv": serv, "helper": helper,
             "gslow": gslow, "gfast": gfast}
 
@@ -193,63 +193,68 @@ def rank_program(g, core, T, topo):
         g.sync.dma_start(T.e_i[:, :], T.idx[:, :]).then_inc(S.s_idx, 16)
         for ch, (a, b) in enumerate(PIECES):
             g.sync.dma_start(T.tabS[:, a:b], T.tab[:, a:b]).then_inc(S["tl%d" % ch], 16)
+        io(T.io128[:, :], [[1, 128]], 0, S.c1)
+        g.iota(T.p_i[:, :], [[0, 1]], 0, 1).then_inc(S.c2, 1)
+        io(T.rowc[:, :], [[0, 4], [CAP, 12]], 0, S.c3)
+        io(T.iom16[:, :], [[0, 8], [1, 16]], 0, S.c4)
+        io(T.ioc4[:, :], [[1, 8], [0, 4]], 0, S.c5)
         V.memset(T.ones_b[:, :], 1.0).then_inc(S.s_ms, 1)
         V.memset(T.opad[:, 0:36], 0.0).then_inc(S.s_ms, 1)
-        io(T.io96[:, :], [[1, 96]], 0, S.cga)
-        io(T.rowc[:, :], [[0, 4], [CAP, 12]], 0, S.cga)
-        g.wait_ge(S.s_ms, 2)
-        g.affine_select(T.ut[:, :], T.ones_b[:, :], [[1, 128]], A.is_gt, 0.0, 0, -1).then_inc(S.cga, 1)
-        io(T.iom16[:, :], [[0, 8], [1, 16]], 0, S.cga)
-        g.iota(T.p_i[:, :], [[0, 1]], 0, 1).then_inc(S.cgb, 1)
-        io(T.ioc4[:, :], [[1, 8], [0, 4]], 0, S.cgb)
+        V.memset(T.keep[:, :], 1.0).then_inc(S.s_k, 1)
+        V.wait_ge(S.s_k, 1)
+        for c in range(4):
+            V.memset(T.keep[:, 12 * c:12 * c + 1], 0.0).then_inc(S.s_k, 1)
+        V.wait_ge(S.c1, 1)
+        V.wait_ge(S.c2, 1)
+        cp(T.p_f[:, :], T.p_i[:, :], S.s_pf)
+        V.wait_ge(S.s_pf, 1)
+        ts(T.ut[:, :], T.io128[:, :], T.p_f[:, 0:1], A.is_gt, S.s_ut)
         V.wait_ge(S.s_idx, 16)
         ts(T.ol_i[:, 0:4], T.e_i[:, :], 12, A.logical_shift_right, S.s1)
         V.wait_ge(S.s1, 1)
         cp(T.ol_f[:, 0:4], T.ol_i[:, 0:4], S.s2)
         V.wait_ge(S.s2, 1)
-        V.wait_ge(S.cga, 4)
         for c in range(4):
-            ts(T.opad[:, 36 + 12 * c:48 + 12 * c], T.io96[:, 0:12], T.ol_f[:, c:c + 1], A.is_equal, S.s3)
+            ts(T.opad[:, 36 + 12 * c:48 + 12 * c], T.io128[:, 0:12], T.ol_f[:, c:c + 1], A.is_equal, S.s3)
         PE.wait_ge(S.s_ms, 2)
-        PE.wait_ge(S.cga, 4)
+        PE.wait_ge(S.c3, 1)
         PE.matmul(T.cnt_ps[:, 0:48], T.ones_b[0:1, :], T.rowc[0:1, :], True, False).then_inc(S.s4, 1)
+        PE.wait_ge(S.s_ut, 1)
         PE.wait_ge(S.s3, 4)
         PE.matmul(T.cnt_ps[:, 0:48], T.ut[:, :], T.opad[:, 36:84], False, False).then_inc(S.s4, 1)
         for s in (1, 2, 3):
             PE.matmul(T.cnt_ps[:, 0:48], T.ones_b[:, :], T.opad[:, 36 - 12 * s:84 - 12 * s], False,
                       s == 3).then_inc(S.s4, 1)
-        ts(T.ol_i[:, 4:8], T.e_i[:, :], RCOL - 64, A.bitwise_and, S.sl1)
-        ts(T.ol_i[:, 8:12], T.e_i[:, :], 63, A.bitwise_and, S.sl1)
-        V.wait_ge(S.sl1, 2)
-        cp(T.ol_f[:, 4:12], T.ol_i[:, 4:12], S.sl2)
+        ts(T.ol_i[:, 4:8], T.e_i[:, :], RCOL - 1, A.bitwise_and, S.sl1)
+        V.wait_ge(S.sl1, 1)
+        ts(T.ol_f[:, 4:8], T.ol_i[:, 4:8], -float(RCOL // 2), A.add, S.sl2)
         V.wait_ge(S.sl2, 1)
+        V.wait_ge(S.s_k, 5)
         V.wait_ge(S.s3, 4)
         V.wait_ge(S.s4, 5)
         V.tensor_tensor(out=T.tmpv[:, :], in0=T.cnt_ps[:, 0:48], in1=T.opad[:, 36:84], op=A.mult).then_inc(S.s5, 1)
         V.wait_ge(S.s5, 1)
-        for c in range(4):
-            V.tensor_reduce(out=T.pos_f[:, c:c + 1], in_=T.tmpv[:, 12 * c:12 * c + 12], axis=AxisListType.X,
-                            op=A.add).then_inc(S.s6, 1)
-        V.wait_ge(S.s6, 4)
-        cp(T.pos_i[:, :], T.pos_f[:, :], S.s7)
+        V.tensor_tensor_scan(out=T.scn[:, :], data0=T.keep[:, :], data1=T.tmpv[:, :], initial=0.0,
+                             op0=A.mult, op1=A.add).then_inc(S.s6, 1)
+        V.wait_ge(S.s6, 1)
+        cp(T.pos_i[:, :], T.scn[:, 11:48:12], S.s7)
         V.wait_ge(S.s7, 1)
         ts(T.hl_i[:, 0:4], T.pos_i[:, :], 15, A.bitwise_and, S.s8)
         ts(T.hl_i[:, 4:8], T.pos_i[:, :], 4, A.logical_shift_right, S.s8)
         V.wait_ge(S.s8, 2)
         cp(T.hl_f[:, :], T.hl_i[:, :], S.s9)
         V.wait_ge(S.s9, 1)
+        V.wait_ge(S.c4, 1)
         for c in range(4):
             sab = S["ab%d" % c]
-            ah, al = T.amat[:, 256 * c:256 * c + 128], T.amat[:, 256 * c + 128:256 * c + 256]
+            am = T.amat[:, 128 * c:128 * c + 128]
             bm = T.bmat[:, 96 * c:96 * c + 96]
-            ts(ah, T.iom16[:, :], T.hl_f[:, c:c + 1], A.is_equal, sab, T.ol_f[:, 4 + c:5 + c], A.mult)
-            ts(al, T.iom16[:, :], T.hl_f[:, c:c + 1], A.is_equal, sab, T.ol_f[:, 8 + c:9 + c], A.mult)
-            ts(bm, T.io96[:, :], T.hl_f[:, 4 + c:5 + c], A.is_equal, sab)
-            PE.wait_ge(sab, 3)
-            PE.matmul(T.rq_ps[:, 0:96], ah, bm, c == 0, False).then_inc(S.s11, 1)
-            PE.matmul(T.rq_ps[:, 0:96], al, bm, False, c == 3).then_inc(S.s11, 1)
-        V.wait_ge(S.s11, 8)
-        cp(T.req[:, :], T.rq_ps[:, 0:96], S.s12)
+            ts(am, T.iom16[:, :], T.hl_f[:, c:c + 1], A.is_equal, sab, T.ol_f[:, 4 + c:5 + c], A.mult)
+            ts(bm, T.io128[:, 0:96], T.hl_f[:, 4 + c:5 + c], A.is_equal, sab)
+            PE.wait_ge(sab, 2)
+            PE.matmul(T.rq_ps[:, 0:96], am, bm, c == 0, c == 3).then_inc(S.s11, 1)
+        V.wait_ge(S.s11, 4)
+        ts(T.req[:, :], T.rq_ps[:, 0:96], float(RCOL // 2), A.add, S.s12)
         V.wait_ge(S.s12, 1)
 
         for ch, (a, b) in enumerate(PIECES):
@@ -283,7 +288,7 @@ def rank_program(g, core, T, topo):
             g.wait_ge(S.gwl, 1)
             pass_on(T.gwf, "hop2", 0, 1)
 
-        V.wait_ge(S.cgb, 2)
+        V.wait_ge(S.c5, 1)
         ts(T.pc_i[:, 0:1], T.p_i[:, :], 7, A.bitwise_and, S.k1)
         ts(T.pc_i[:, 1:2], T.p_i[:, :], 3, A.logical_shift_right, S.k1)
         V.wait_ge(S.k1, 2)
@@ -293,7 +298,7 @@ def rank_program(g, core, T, topo):
         ts(T.l2[:, :], T.iom16[:, :], T.pc_f[:, 1:2], A.is_equal, S.k3)
         V.wait_ge(S.k3, 2)
         for c in range(4):
-            ts(T.rhs2[:, c:32:4], T.mk[:, c:32:4], T.pos_f[:, c:c + 1], A.mult, S.s13)
+            ts(T.rhs2[:, c:32:4], T.mk[:, c:32:4], T.scn[:, 12 * c + 11:12 * c + 12], A.mult, S.s13)
         PE.wait_ge(S.k3, 2)
         PE.wait_ge(S.s13, 4)
         PE.matmul(T.po_ps[:, 0:32], T.l2[:, :], T.rhs2[:, :], True, True).then_inc(S.s14, 1)

from concourse.bass import DstId, RemoteDMATransfer
from concourse.mybir import AluOpType, ActivationFunctionType

RCOL = 4096
CAP = 128
NENT = 512
W8 = CAP // 16
PIECES = [(0, 1024), (1024, 2048), (2048, 3072), (3072, RCOL)]
FSPLIT = 2
NCH = len(PIECES)

_F, _B, _I, _U, _H = "float32", "bfloat16", "int32", "uint16", "float16"
SCRATCH = {n: ("sbuf", [128, w], d) for (n, w, d) in [
    ("tabS", RCOL, _B), ("e_i", 4, _I), ("ol_i", 8, _I), ("ol_f", 8, _F), ("opad", 84, _B), ("ones_b", 128, _B),
    ("ut", 128, _B), ("rowc", 48, _B), ("io128", 128, _B), ("iom16", 128, _B), ("ioc4", 32, _F), ("p_i", 1, _I),
    ("p_f", 1, _F), ("pc_i", 2, _I), ("pc_f", 2, _F), ("mk", 32, _F), ("l2", 128, _F), ("tmpv", 48, _F),
    ("keep", 48, _F), ("scn", 48, _F), ("pos_i", 4, _I), ("hl_i", 8, _I), ("hl_f", 8, _F), ("amat", 512, _H),
    ("bmat", 384, _H), ("req", 96, _U), ("rhs2", 32, _F), ("posoff", 32, _U), ("gw", 72, _U), ("gwf", 72, _U),
    ("rq", 288, _U), ("rep", 1536, _B), ("land", 1536, _B), ("yS", NENT, _B)]}
SCRATCH.update({n: ("psum", [128, 512], _F) for n in ("cnt_ps", "rq_ps", "po_ps")})
SEMAPHORES = (["s_idx", "s_ms", "s_k", "c1", "c2", "c3", "c4", "c5", "s_pf", "s_ut", "k1", "k2", "k3", "sl1", "sl2",
               "ab0", "ab1", "ab2", "ab3"]
              + ["s%d" % i for i in range(1, 16)]
              + ["gwin", "gwfin", "gwl", "tabin", "rq0", "rq1", "rq2", "rq3", "got", "sent", "selfg"]
              + ["gth%d" % i for i in range(6)] + ["tl%d" % i for i in range(NCH)]
              + ["fin%d" % i for i in range(FSPLIT)] + ["yd%d" % i for i in range(FSPLIT)])


def _bits(m):
    return [b for b in range(32) if (m >> b) & 1]


def _mk(eng):
    return sum(1 << b for b in eng)


def _plan(cores, topo):
    chips = []
    for c in cores:
        if topo.chip(c) not in chips:
            chips.append(topo.chip(c))
    allc = range(max(cores) + 1)
    on = {X: [c for c in allc if topo.chip(c) == X] for X in chips}
    rk = {X: [c for c in cores if topo.chip(c) == X] for X in chips}
    m = len(rk[chips[0]])
    for ci, X in enumerate(chips):
        assert len(rk[X]) == m
        for i, c in enumerate(rk[X]):
            assert cores.index(c) == ci * m + i

    def rel(X, Y):
        if X == Y:
            return "own"
        if topo.mates(X, Y):
            return "mate"
        if topo.same_plane(X, Y):
            return "plane"
        return "hop2"

    serv, helper, gslow, gfast = {}, {}, {}, {}
    for X in chips:
        far = rk[[Y for Y in chips if topo.mates(X, Y)][0]][0]
        ports = [c for c in on[X] if topo.may_write(c, far)]
        used = []
        for k in sorted(range(m), key=lambda k: rk[X][k] in ports):
            c = rk[X][k]
            free = [h for h in ports if h not in rk[X] and h not in used]
            if c in ports:
                h = sorted(free, key=lambda h: (topo.die(h) == topo.die(c), h))[0]
                serv[(X, k)] = {"own": c, "plane": c, "mate": c, "hop2": h}
            else:
                h = sorted(free, key=lambda h: (topo.die(h) != topo.die(c), h))[0]
                serv[(X, k)] = {"own": c, "plane": c, "mate": h, "hop2": h}
            used.append(h)
            helper[(X, k)] = h
        gslow[X] = [helper[(X, k)] for k in range(m)]
        gfast[X] = [c for c in rk[X] if c in ports][0]
    return {"chips": chips, "on": on, "rk": rk, "m": m, "rel": rel, "serv": serv, "helper": helper,
            "gslow": gslow, "gfast": gfast}


def _engines(core, PL, topo):
    X = topo.chip(core)
    near = [c for c in PL["on"][X] if c != core][0]
    far = PL["rk"][[Y for Y in PL["chips"] if Y != X][0]][0]
    lo = _bits(topo.mask(core, far))
    hi = [b for b in _bits(topo.mask(core, near)) if b not in lo]
    return lo, hi


def _table_of(core, PL, topo):
    X = topo.chip(core)
    for k in range(PL["m"]):
        if PL["rk"][X][k] == core or PL["helper"][(X, k)] == core:
            return k
    return None


def _sched(core, PL, topo):
    Y = topo.chip(core)
    k = _table_of(core, PL, topo)
    if k is None:
        return []
    lo, hi = _engines(core, PL, topo)
    sv = PL["serv"][(Y, k)]
    calls = []
    if sv["own"] == core:
        own = [(Y, i) for i in range(PL["m"]) if i != k]
        n = len(hi) // 2
        calls.append([(own[j][0], own[j][1], hi[j * n:(j + 1) * n]) for j in range(len(own))])
    h = len(lo) // 2
    for r in ("plane", "hop2", "mate"):
        if sv[r] != core:
            continue
        off = [(X, i) for X in PL["chips"] if PL["rel"](Y, X) == r for i in range(PL["m"])]
        j = 0
        while j < len(off):
            if j + 1 < len(off):
                calls.append([(off[j][0], off[j][1], lo[:h]), (off[j + 1][0], off[j + 1][1], lo[h:])])
                j += 2
            else:
                calls.append([(off[j][0], off[j][1], lo)])
                j += 1
    return calls


def rank_program(g, core, T, topo):
    cores = list(T.cores)
    PL = _plan(cores, topo)
    X = topo.chip(core)
    if X not in PL["chips"]:
        return
    chips, rk, m, rel = PL["chips"], PL["rk"], PL["m"], PL["rel"]
    SL = W8 * m
    BL = SL * m
    rank = T.rank_of(core)
    ktab = _table_of(core, PL, topo)
    if rank is None and ktab is None:
        return
    V, PE, S, AC = g.vector, g.tensor, T.sem, g.scalar
    lo, hi = _engines(core, PL, topo)
    gslow, gfast = PL["gslow"][X], PL["gfast"][X]
    ciX = chips.index(X)
    sent = [0]
    A = AluOpType

    def send(trs):
        L = []
        for (src, dsts, eng, sem) in trs:
            ids, aps = [], []
            for (d, ap) in dsts:
                assert topo.may_write(core, d) and (_mk(eng) & ~topo.mask(core, d)) == 0
                a = topo.addr(d)
                ids.append(DstId(rid=a[0], pnc=a[1]))
                aps.append(ap)
            L.append(RemoteDMATransfer(dst_ids=ids, dma_engine_mask=_mk(eng), remote_sem=sem,
                                       srcs=[src], dsts=aps, alu_op=0))
            sent[0] += len(eng)
        g.remote_dma_fused(L, local_sem=S.sent)

    def uniq(seq):
        out = []
        for c in seq:
            if c not in out:
                out.append(c)
        return out

    def ts(out, in0, s1, op0, sem, s2=None, op1=None):
        if op1 is None:
            V.tensor_scalar(out=out, in0=in0, scalar1=s1, scalar2=None, op0=op0).then_inc(sem, 1)
        else:
            V.tensor_scalar(out=out, in0=in0, scalar1=s1, scalar2=s2, op0=op0, op1=op1).then_inc(sem, 1)

    def cp(out, in_, sem):
        V.tensor_copy(out=out, in_=in_).then_inc(sem, 1)

    def gather(q, out, in_, sem):
        if q is V:
            V.tensor_copy(out=out, in_=in_).then_inc(sem, 1)
        else:
            AC.activation(out=out, in_=in_, func=ActivationFunctionType.Copy, bias=-0.0, scale=1.0).then_inc(sem, 1)

    def io(out, pat, cm, sem):
        g.iota(out, pat, 0, cm, allow_small_or_imprecise_dtypes=True).then_inc(sem, 1)

    def pass_on(buf, r, part, of):
        Y = [Z for Z in chips if rel(X, Z) == r][0]
        ds = uniq([PL["serv"][(Y, k)][r] for k in range(m)])[part::of]
        send([(buf[:, 0:BL], [(d, T.rq[:, ciX * BL:(ciX + 1) * BL]) for d in ds], lo, S["rq%d" % ciX])])

    if rank is not None:
        i_me = rk[X].index(core)
        g.sync.dma_start(T.e_i[:, :], T.idx[:, :]).then_inc(S.s_idx, 16)
        for ch, (a, b) in enumerate(PIECES):
            g.sync.dma_start(T.tabS[:, a:b], T.tab[:, a:b]).then_inc(S["tl%d" % ch], 16)
        io(T.io128[:, :], [[1, 128]], 0, S.c1)
        g.iota(T.p_i[:, :], [[0, 1]], 0, 1).then_inc(S.c2, 1)
        io(T.rowc[:, :], [[0, 4], [CAP, 12]], 0, S.c3)
        io(T.iom16[:, :], [[0, 8], [1, 16]], 0, S.c4)
        io(T.ioc4[:, :], [[1, 8], [0, 4]], 0, S.c5)
        V.memset(T.ones_b[:, :], 1.0).then_inc(S.s_ms, 1)
        V.memset(T.opad[:, 0:36], 0.0).then_inc(S.s_ms, 1)
        V.memset(T.keep[:, :], 1.0).then_inc(S.s_k, 1)
        V.wait_ge(S.s_k, 1)
        for c in range(4):
            V.memset(T.keep[:, 12 * c:12 * c + 1], 0.0).then_inc(S.s_k, 1)
        V.wait_ge(S.c1, 1)
        V.wait_ge(S.c2, 1)
        cp(T.p_f[:, :], T.p_i[:, :], S.s_pf)
        V.wait_ge(S.s_pf, 1)
        ts(T.ut[:, :], T.io128[:, :], T.p_f[:, 0:1], A.is_gt, S.s_ut)
        V.wait_ge(S.s_idx, 16)
        ts(T.ol_i[:, 0:4], T.e_i[:, :], 12, A.logical_shift_right, S.s1)
        V.wait_ge(S.s1, 1)
        cp(T.ol_f[:, 0:4], T.ol_i[:, 0:4], S.s2)
        V.wait_ge(S.s2, 1)
        for c in range(4):
            ts(T.opad[:, 36 + 12 * c:48 + 12 * c], T.io128[:, 0:12], T.ol_f[:, c:c + 1], A.is_equal, S.s3)
        PE.wait_ge(S.s_ms, 2)
        PE.wait_ge(S.c3, 1)
        PE.matmul(T.cnt_ps[:, 0:48], T.ones_b[0:1, :], T.rowc[0:1, :], True, False).then_inc(S.s4, 1)
        PE.wait_ge(S.s_ut, 1)
        PE.wait_ge(S.s3, 4)
        PE.matmul(T.cnt_ps[:, 0:48], T.ut[:, :], T.opad[:, 36:84], False, False).then_inc(S.s4, 1)
        for s in (1, 2, 3):
            PE.matmul(T.cnt_ps[:, 0:48], T.ones_b[:, :], T.opad[:, 36 - 12 * s:84 - 12 * s], False,
                      s == 3).then_inc(S.s4, 1)
        ts(T.ol_i[:, 4:8], T.e_i[:, :], RCOL - 1, A.bitwise_and, S.sl1)
        V.wait_ge(S.sl1, 1)
        ts(T.ol_f[:, 4:8], T.ol_i[:, 4:8], -float(RCOL // 2), A.add, S.sl2)
        V.wait_ge(S.sl2, 1)
        V.wait_ge(S.s_k, 5)
        V.wait_ge(S.s3, 4)
        V.wait_ge(S.s4, 5)
        V.tensor_tensor(out=T.tmpv[:, :], in0=T.cnt_ps[:, 0:48], in1=T.opad[:, 36:84], op=A.mult).then_inc(S.s5, 1)
        V.wait_ge(S.s5, 1)
        V.tensor_tensor_scan(out=T.scn[:, :], data0=T.keep[:, :], data1=T.tmpv[:, :], initial=0.0,
                             op0=A.mult, op1=A.add).then_inc(S.s6, 1)
        V.wait_ge(S.s6, 1)
        cp(T.pos_i[:, :], T.scn[:, 11:48:12], S.s7)
        V.wait_ge(S.s7, 1)
        ts(T.hl_i[:, 0:4], T.pos_i[:, :], 15, A.bitwise_and, S.s8)
        ts(T.hl_i[:, 4:8], T.pos_i[:, :], 4, A.logical_shift_right, S.s8)
        V.wait_ge(S.s8, 2)
        cp(T.hl_f[:, :], T.hl_i[:, :], S.s9)
        V.wait_ge(S.s9, 1)
        V.wait_ge(S.c4, 1)
        for c in range(4):
            sab = S["ab%d" % c]
            am = T.amat[:, 128 * c:128 * c + 128]
            bm = T.bmat[:, 96 * c:96 * c + 96]
            ts(am, T.iom16[:, :], T.hl_f[:, c:c + 1], A.is_equal, sab, T.ol_f[:, 4 + c:5 + c], A.mult)
            ts(bm, T.io128[:, 0:96], T.hl_f[:, 4 + c:5 + c], A.is_equal, sab)
            PE.wait_ge(sab, 2)
            PE.matmul(T.rq_ps[:, 0:96], am, bm, c == 0, c == 3).then_inc(S.s11, 1)
        V.wait_ge(S.s11, 4)
        ts(T.req[:, :], T.rq_ps[:, 0:96], float(RCOL // 2), A.add, S.s12)
        V.wait_ge(S.s12, 1)

        for ch, (a, b) in enumerate(PIECES):
            g.wait_ge(S["tl%d" % ch], 16)
            send([(T.tabS[:, a:b], [(PL["helper"][(X, i_me)], T.tabS[:, a:b])], lo + hi, S.tabin)])
        g.wait_ge(S.s12, 1)
        first, second = [], []
        mine = slice(i_me * SL, (i_me + 1) * SL)
        for Y in chips:
            ciY = chips.index(Y)
            src = T.req[:, ciY * SL:(ciY + 1) * SL]
            r = rel(X, Y)
            dcol = ciX * BL + i_me * SL
            if r == "mate":
                first.append((src, [(d, T.gw[:, mine]) for d in gslow], lo, S.gwin))
            elif r == "hop2":
                if core == gfast:
                    cp(T.gwf[:, mine], src, S.gwl)
                else:
                    first.append((src, [(gfast, T.gwf[:, mine])], hi, S.gwfin))
            elif r == "plane":
                ds = uniq([PL["serv"][(Y, k)]["plane"] for k in range(m)])
                second.append((src, [(d, T.rq[:, dcol:dcol + SL]) for d in ds], lo, S["rq%d" % ciX]))
            else:
                ds = [c for c in rk[X] if c != core]
                second.append((src, [(d, T.rq[:, dcol:dcol + SL]) for d in ds], hi, S["rq%d" % ciX]))
        send(first)
        send(second)
        if core == gfast:
            g.wait_ge(S.gwfin, (m - 1) * len(hi))
            g.wait_ge(S.gwl, 1)
            pass_on(T.gwf, "hop2", 0, 1)

        V.wait_ge(S.c5, 1)
        ts(T.pc_i[:, 0:1], T.p_i[:, :], 7, A.bitwise_and, S.k1)
        ts(T.pc_i[:, 1:2], T.p_i[:, :], 3, A.logical_shift_right, S.k1)
        V.wait_ge(S.k1, 2)
        cp(T.pc_f[:, :], T.pc_i[:, :], S.k2)
        V.wait_ge(S.k2, 1)
        ts(T.mk[:, :], T.ioc4[:, :], T.pc_f[:, 0:1], A.is_equal, S.k3)
        ts(T.l2[:, :], T.iom16[:, :], T.pc_f[:, 1:2], A.is_equal, S.k3)
        V.wait_ge(S.k3, 2)
        for c in range(4):
            ts(T.rhs2[:, c:32:4], T.mk[:, c:32:4], T.scn[:, 12 * c + 11:12 * c + 12], A.mult, S.s13)
        PE.wait_ge(S.k3, 2)
        PE.wait_ge(S.s13, 4)
        PE.matmul(T.po_ps[:, 0:32], T.l2[:, :], T.rhs2[:, :], True, True).then_inc(S.s14, 1)
        V.wait_ge(S.s14, 1)
        cp(T.posoff[:, :], T.po_ps[:, 0:32], S.s15)
        for q in (V, AC):
            for ch in range(NCH):
                q.wait_ge(S["tl%d" % ch], 16)
        cp(T.land[:, rank * CAP:(rank + 1) * CAP],
           T.tabS[:, 0:RCOL].indirect(T.req[:, rank * W8:(rank + 1) * W8]), S.selfg)
    else:
        for q in (V, AC):
            q.wait_ge(S.tabin, NCH * (len(lo) + len(hi)))

    if core in gslow:
        g.wait_ge(S.gwin, m * len(lo))
        pass_on(T.gw, "mate", gslow.index(core), len(gslow))

    owner = ciX * m + ktab
    waited = {0: [], 1: []}
    nb = 0
    for n, call in enumerate(_sched(core, PL, topo)):
        trs = []
        for (Z, i, eng) in call:
            ciZ = chips.index(Z)
            q = (V, AC)[nb % 2]
            if ciZ not in waited[nb % 2]:
                r = rel(X, Z)
                tot = {"own": (m - 1) * len(hi), "plane": m * len(lo), "mate": len(lo), "hop2": len(lo)}[r]
                q.wait_ge(S["rq%d" % ciZ], tot)
                waited[nb % 2].append(ciZ)
            rr = ciZ * m + i
            col = ciZ * BL + i * SL + ktab * W8
            gather(q, T.rep[:, rr * CAP:(rr + 1) * CAP], T.tabS[:, 0:RCOL].indirect(T.rq[:, col:col + W8]),
                   S["gth%d" % n])
            nb += 1
            trs.append((T.rep[:, rr * CAP:(rr + 1) * CAP],
                        [(rk[Z][i], T.land[:, owner * CAP:(owner + 1) * CAP])], eng, S.got))
        g.wait_ge(S["gth%d" % n], len(call))
        send(trs)

    if rank is not None:
        tot = 0
        for Z in chips:
            for c in PL["on"][Z]:
                for call in _sched(c, PL, topo):
                    for (Q, i, eng) in call:
                        if rk[Q][i] == core:
                            tot += len(eng)
        FW = NENT // FSPLIT
        for f in range(FSPLIT):
            q, d = ((V, g.sync), (AC, g.scalar))[f % 2]
            q.wait_ge(S.got, tot)
            q.wait_ge(S.selfg, 1)
            q.wait_ge(S.s15, 1)
            gather(q, T.yS[:, f * FW:(f + 1) * FW],
                   T.land[:, 0:12 * CAP].indirect(T.posoff[:, f * FW // 16:(f + 1) * FW // 16]), S["fin%d" % f])
            d.wait_ge(S["fin%d" % f], 1)
            d.dma_start(T.y[:, f * FW:(f + 1) * FW], T.yS[:, f * FW:(f + 1) * FW]).then_inc(S["yd%d" % f], 16)
            d.wait_ge(S["yd%d" % f], 16)
    if sent[0]:
        g.wait_ge(S.sent, sent[0])
